import numpy as np, ml_dtypes
CORES = [16,17,18,19,150,151]
N = 6
import mx_ref
NC = 128
BF = ml_dtypes.bfloat16
def cut(t, i, w=512):
    return t[:, w * i:w * i + w]
def pk(c, s, i=0):
    return (np.ascontiguousarray(c[:, 512 * i:512 * i + 512]), mx_ref.live(s[:, 128 * i:128 * i + 128]))
def inputs(rng, e, E):
    def f(*shape):
        v = (rng.standard_normal(shape, dtype=np.float32) * np.exp2(rng.integers(-2, 3, shape[:-1] + (1,)))).astype(BF)
        return mx_ref.spread((v.astype(np.float32) * np.exp2(rng.integers(-E, E + 1, shape[:-2] + (1, 1))).astype(np.float32)).astype(BF), rng, e)
    def packed(k):
        c = np.zeros((N, 128, k * 512), np.uint8); s = np.zeros((N, 128, k * 128), np.uint8)
        for r in range(N):
            for i in range(k):
                a, b = mx_ref.quantize(f(128, 512)); c[r][:, 512 * i:512 * i + 512] = a; s[r][:, 128 * i:128 * i + 128] = mx_ref.plane(b, rng)
        return c, s
    d = {}
    d["wc"], d["ws"] = packed(N)
    d["x"] = f(N, 128, N * 4 * NC)
    return d
def setup_inputs(rng):
    return inputs(rng, 0, 0)
def setup_inputs_blocks(rng):
    return inputs(rng, 2, 0)
def setup_inputs_wide(rng):
    return inputs(rng, 0, 8)
def reference(wc, ws, x):
    y = np.zeros((N, 128, NC), np.float32)
    for r in range(N):
        for j in range(N):
            p = mx_ref.matmul(pk(wc[j], ws[j], r), mx_ref.quantize(cut(x[r], j, 4 * NC)))
            y[r] = p if j == 0 else y[r] + p
    return {"y": y}

@@ -1,0 +1,122 @@
+from concourse.bass import DstId, RemoteDMATransfer
+from concourse.mybir import dt
+
+N = 6
+W = 128
+
+SCRATCH = {
+    "wq": ("sbuf", [128, N * W], "float8_e4m3fn_x4"),
+    "wp": ("sbuf", [128, N * W], "uint8"),
+    "rq": ("sbuf", [128, (N - 1) * W], "float8_e4m3fn_x4"),
+    "rp": ("sbuf", [128, (N - 1) * W], "uint8"),
+    "xb": ("sbuf", [128, N * 4 * W], "bfloat16"),
+    "xq": ("sbuf", [128, N * W], "float8_e4m3fn_x4"),
+    "xp": ("sbuf", [128, N * W], "uint8"),
+    "acc": ("psum", [128, 512], "float32"),
+    "yb": ("sbuf", [128, W], "float32"),
+}
+SEMAPHORES = ["ldp", "ldc", "ldx0", "ldx1", "q0", "q1", "sent", "mm", "cp", "st"] + ["a%d" % j for j in range(N)]
+
+
+def _engines(mask):
+    return [e for e in range(mask.bit_length()) if (mask >> e) & 1]
+
+
+def _shares(engines, k):
+    n = 1
+    while 2 * n * k <= len(engines):
+        n *= 2
+    sizes = [n] * k
+    free = len(engines) - n * k
+    for i in range(k):
+        if free >= sizes[i]:
+            free -= sizes[i]
+            sizes[i] *= 2
+    runs, at = [], 0
+    for s in sizes:
+        runs.append(engines[at:at + s])
+        at += s
+    return runs
+
+
+def _split(j, cores, topo):
+    def place(c):
+        return (topo.host(c), topo.chip(c))
+    others = [(j + k) % N for k in range(1, N)]
+    far = [d for d in others if place(cores[d]) != place(cores[j])]
+    near = [d for d in others if place(cores[d]) == place(cores[j])]
+    return far, near
+
+
+def _lanes(j, cores, topo):
+    far, near = _split(j, cores, topo)
+    out = _engines(topo.mask(cores[j], cores[far[0]]))
+    home = [e for e in _engines(topo.mask(cores[j], cores[near[0]])) if e not in out]
+    lanes = {}
+    for group, engines in ((far, out), (near, home)):
+        for d, run in zip(group, _shares(engines, len(group))):
+            lanes[d] = run
+    return lanes
+
+
+def rank_program(g, core, T, topo):
+    r = T.rank_of(core)
+    if r is None:
+        return
+    cores, S, u8 = list(T.cores), T.sem, dt.uint8
+    half = N * W // 2
+
+    def tile(buf, i):
+        return buf[:, W * i:W * i + W]
+
+    def slot(j, at):
+        return j if j < at else j - 1
+
+    g.sync.dma_start(T.wp[:], T.ws[:]).then_inc(S.ldp, 16)
+    g.scalar.dma_start(T.wq[:].bitcast(u8), T.wc[:]).then_inc(S.ldc, 16)
+    g.sync.dma_start(T.xb[:, 0:4 * half], T.x[:, 0:4 * half]).then_inc(S.ldx0, 16)
+    g.scalar.dma_start(T.xb[:, 4 * half:8 * half], T.x[:, 4 * half:8 * half]).then_inc(S.ldx1, 16)
+
+    far, near = _split(r, cores, topo)
+    lanes = _lanes(r, cores, topo)
+    planes, codes, left = [], [], 0
+    for d in far + near:
+        rid, pid = topo.addr(cores[d], core)
+        mask = sum(1 << e for e in lanes[d])
+        to = dict(dst_ids=[DstId(rid=rid, pnc=pid)], dma_engine_mask=mask, remote_sem=S["a%d" % r])
+        planes.append(RemoteDMATransfer(src=tile(T.wp, d), dst=tile(T.rp, slot(r, d)), **to))
+        codes.append(RemoteDMATransfer(src=tile(T.wq, d).bitcast(u8), dst=tile(T.rq, slot(r, d)).bitcast(u8), **to))
+        left += 2 * len(lanes[d])
+    g.wait_ge(S.ldp, 16)
+    g.remote_dma_fused(planes, local_sem=S.sent)
+    g.wait_ge(S.ldc, 16)
+    g.remote_dma_fused(codes, local_sem=S.sent)
+
+    for h, (ld, q) in enumerate(((S.ldx0, S.q0), (S.ldx1, S.q1))):
+        g.vector.wait_ge(ld, 16)
+        g.vector.quantize_mx(T.xq[:, half * h:half * h + half], T.xp[:, half * h:half * h + half],
+                             T.xb[:, 4 * half * h:4 * half * h + 4 * half]).then_inc(q, 1)
+
+    order = [r] + near + far
+    seen = set()
+    for i, j in enumerate(order):
+        h = (W * j) // half
+        if h not in seen:
+            seen.add(h)
+            g.tensor.wait_ge((S.q0, S.q1)[h], 1)
+        if j == r:
+            g.tensor.wait_ge(S.ldp, 16)
+            g.tensor.wait_ge(S.ldc, 16)
+            wq, wp = tile(T.wq, r), tile(T.wp, r)
+        else:
+            g.tensor.wait_ge(S["a%d" % j], 2 * len(_lanes(j, cores, topo)[r]))
+            wq, wp = tile(T.rq, slot(j, r)), tile(T.rp, slot(j, r))
+        mm = g.tensor.matmul_mx(T.acc[:, 0:W], wq, wp, tile(T.xq, j), tile(T.xp, j), i == 0, i == N - 1)
+    mm.then_inc(S.mm, 1)
+
+    g.vector.wait_ge(S.mm, 1)
+    g.vector.tensor_copy(T.yb[:], T.acc[:, 0:W]).then_inc(S.cp, 1)
+    g.sync.wait_ge(S.cp, 1)
+    g.sync.dma_start(T.y[:], T.yb[:]).then_inc(S.st, 16)
+    g.sync.wait_ge(S.st, 16)
+    g.wait_ge(S.sent, left)

@@ -3,6 +3,7 @@ from concourse.mybir import dt
 
 N = 6
 W = 128
+WORLD = 256
 
 SCRATCH = {
     "wq": ("sbuf", [128, N * W], "float8_e4m3fn_x4"),
@@ -15,7 +16,8 @@ SCRATCH = {
     "acc": ("psum", [128, 512], "float32"),
     "yb": ("sbuf", [128, W], "float32"),
 }
-SEMAPHORES = ["ldp", "ldc", "ldx0", "ldx1", "q0", "q1", "sent", "mm", "cp", "st"] + ["a%d" % j for j in range(N)]
+SEMAPHORES = (["ldp", "ldc", "ldx0", "ldx1", "q0", "q1", "sent", "mm", "cp", "st", "pa", "ca"]
+              + ["a%d" % j for j in range(N)])
 
 
 def _engines(mask):
@@ -39,32 +41,51 @@ def _shares(engines, k):
     return runs
 
 
+def _place(c, topo):
+    return (topo.host(c), topo.chip(c))
+
+
 def _split(j, cores, topo):
-    def place(c):
-        return (topo.host(c), topo.chip(c))
     others = [(j + k) % N for k in range(1, N)]
-    far = [d for d in others if place(cores[d]) != place(cores[j])]
-    near = [d for d in others if place(cores[d]) == place(cores[j])]
+    far = [d for d in others if _place(cores[d], topo) != _place(cores[j], topo)]
+    near = [d for d in others if _place(cores[d], topo) == _place(cores[j], topo)]
     return far, near
 
 
-def _lanes(j, cores, topo):
+def _routes(cores, topo):
+    routes, taken = {}, set(cores)
+    for j in range(N):
+        far, _ = _split(j, cores, topo)
+        for i, d in enumerate(far):
+            if (i + j) % 2:
+                continue
+            spare = [c for c in range(WORLD) if c not in taken and _place(c, topo) == _place(cores[j], topo)
+                     and topo.die(c) != topo.die(cores[j]) and topo.may_write(c, cores[d])]
+            if spare:
+                routes[(j, d)] = spare[0]
+                taken.add(spare[0])
+    return routes
+
+
+def _lanes(j, cores, topo, routes):
     far, near = _split(j, cores, topo)
+    direct = [d for d in far if (j, d) not in routes]
+    relayed = [d for d in far if (j, d) in routes]
+    every = _engines(topo.mask(cores[j], cores[near[0]]))
     out = _engines(topo.mask(cores[j], cores[far[0]]))
-    home = [e for e in _engines(topo.mask(cores[j], cores[near[0]])) if e not in out]
+    home = [e for e in every if e not in out]
     lanes = {}
-    for group, engines in ((far, out), (near, home)):
-        for d, run in zip(group, _shares(engines, len(group))):
-            lanes[d] = run
+    for group, engines in ((direct, out), (relayed, home), (near, every)):
+        if group:
+            for d, run in zip(group, _shares(engines, len(group))):
+                lanes[d] = run
     return lanes
 
 
 def rank_program(g, core, T, topo):
-    r = T.rank_of(core)
-    if r is None:
-        return
     cores, S, u8 = list(T.cores), T.sem, dt.uint8
-    half = N * W // 2
+    routes = _routes(cores, topo)
+    r = T.rank_of(core)
 
     def tile(buf, i):
         return buf[:, W * i:W * i + W]
@@ -72,32 +93,60 @@ def rank_program(g, core, T, topo):
     def slot(j, at):
         return j if j < at else j - 1
 
+    def write(src_core, dst_core, engines, sem, src, dst):
+        rid, pid = topo.addr(dst_core, src_core)
+        return RemoteDMATransfer(src=src, dst=dst, dst_ids=[DstId(rid=rid, pnc=pid)],
+                                 dma_engine_mask=sum(1 << e for e in engines), remote_sem=sem)
+
+    if r is None:
+        for (j, d), c in routes.items():
+            if c != core:
+                continue
+            came = len(_lanes(j, cores, topo, routes)[d])
+            on = _engines(topo.mask(core, cores[d]))
+            g.wait_ge(S.pa, came)
+            g.remote_dma_fused([write(core, cores[d], on, S["a%d" % j], tile(T.rp, 0), tile(T.rp, slot(j, d)))],
+                               local_sem=S.sent)
+            g.wait_ge(S.ca, came)
+            g.remote_dma_fused([write(core, cores[d], on, S["a%d" % j], tile(T.rq, 0).bitcast(u8),
+                                      tile(T.rq, slot(j, d)).bitcast(u8))], local_sem=S.sent)
+            g.wait_ge(S.sent, 2 * len(on))
+        return
+
+    half = N * W // 2
+
     g.sync.dma_start(T.wp[:], T.ws[:]).then_inc(S.ldp, 16)
     g.scalar.dma_start(T.wq[:].bitcast(u8), T.wc[:]).then_inc(S.ldc, 16)
     g.sync.dma_start(T.xb[:, 0:4 * half], T.x[:, 0:4 * half]).then_inc(S.ldx0, 16)
     g.scalar.dma_start(T.xb[:, 4 * half:8 * half], T.x[:, 4 * half:8 * half]).then_inc(S.ldx1, 16)
 
     far, near = _split(r, cores, topo)
-    lanes = _lanes(r, cores, topo)
-    planes, codes, left = [], [], 0
-    for d in far + near:
-        rid, pid = topo.addr(cores[d], core)
-        mask = sum(1 << e for e in lanes[d])
-        to = dict(dst_ids=[DstId(rid=rid, pnc=pid)], dma_engine_mask=mask, remote_sem=S["a%d" % r])
-        planes.append(RemoteDMATransfer(src=tile(T.wp, d), dst=tile(T.rp, slot(r, d)), **to))
-        codes.append(RemoteDMATransfer(src=tile(T.wq, d).bitcast(u8), dst=tile(T.rq, slot(r, d)).bitcast(u8), **to))
-        left += 2 * len(lanes[d])
+    lanes = _lanes(r, cores, topo, routes)
+    calls = {}
+    for name, group in (("far", far), ("near", near)):
+        planes, codes = [], []
+        for d in group:
+            if (r, d) in routes:
+                to, at, sp, sc = routes[(r, d)], 0, S.pa, S.ca
+            else:
+                to, at, sp, sc = cores[d], slot(r, d), S["a%d" % r], S["a%d" % r]
+            planes.append(write(core, to, lanes[d], sp, tile(T.wp, d), tile(T.rp, at)))
+            codes.append(write(core, to, lanes[d], sc, tile(T.wq, d).bitcast(u8), tile(T.rq, at).bitcast(u8)))
+        calls[name] = (planes, codes)
+    left = 2 * sum(len(lanes[d]) for d in far + near)
     g.wait_ge(S.ldp, 16)
-    g.remote_dma_fused(planes, local_sem=S.sent)
+    g.remote_dma_fused(calls["far"][0], local_sem=S.sent)
+    g.remote_dma_fused(calls["near"][0], local_sem=S.sent)
     g.wait_ge(S.ldc, 16)
-    g.remote_dma_fused(codes, local_sem=S.sent)
+    g.remote_dma_fused(calls["far"][1], local_sem=S.sent)
+    g.remote_dma_fused(calls["near"][1], local_sem=S.sent)
 
     for h, (ld, q) in enumerate(((S.ldx0, S.q0), (S.ldx1, S.q1))):
         g.vector.wait_ge(ld, 16)
         g.vector.quantize_mx(T.xq[:, half * h:half * h + half], T.xp[:, half * h:half * h + half],
                              T.xb[:, 4 * half * h:4 * half * h + 4 * half]).then_inc(q, 1)
 
-    order = [r] + near + far
+    order = [r] + near + [j for j in far if (j, r) not in routes] + [j for j in far if (j, r) in routes]
     seen = set()
     for i, j in enumerate(order):
         h = (W * j) // half
@@ -109,7 +158,11 @@ def rank_program(g, core, T, topo):
             g.tensor.wait_ge(S.ldc, 16)
             wq, wp = tile(T.wq, r), tile(T.wp, r)
         else:
-            g.tensor.wait_ge(S["a%d" % j], 2 * len(_lanes(j, cores, topo)[r]))
+            if (j, r) in routes:
+                n = len(_engines(topo.mask(routes[(j, r)], core)))
+            else:
+                n = len(_lanes(j, cores, topo, routes)[r])
+            g.tensor.wait_ge(S["a%d" % j], 2 * n)
             wq, wp = tile(T.rq, slot(j, r)), tile(T.rp, slot(j, r))
         mm = g.tensor.matmul_mx(T.acc[:, 0:W], wq, wp, tile(T.xq, j), tile(T.xp, j), i == 0, i == N - 1)
     mm.then_inc(S.mm, 1)

from concourse.bass import DstId, RemoteDMATransfer
from concourse.mybir import dt

N = 6
W = 128
WORLD = 256

SCRATCH = {
    "wq": ("sbuf", [128, N * W], "float8_e4m3fn_x4"),
    "wp": ("sbuf", [128, N * W], "uint8"),
    "rq": ("sbuf", [128, (N - 1) * W], "float8_e4m3fn_x4"),
    "rp": ("sbuf", [128, (N - 1) * W], "uint8"),
    "xb": ("sbuf", [128, N * 4 * W], "bfloat16"),
    "xq": ("sbuf", [128, N * W], "float8_e4m3fn_x4"),
    "xp": ("sbuf", [128, N * W], "uint8"),
    "acc": ("psum", [128, 512], "float32"),
    "yb": ("sbuf", [128, W], "float32"),
}
SEMAPHORES = (["ldp", "ldc", "ldx0", "ldx1", "q0", "q1", "sent", "mm", "cp", "st", "pa", "ca"]
              + ["a%d" % j for j in range(N)])


def _engines(mask):
    return [e for e in range(mask.bit_length()) if (mask >> e) & 1]


def _shares(engines, k):
    n = 1
    while 2 * n * k <= len(engines):
        n *= 2
    sizes = [n] * k
    free = len(engines) - n * k
    for i in range(k):
        if free >= sizes[i]:
            free -= sizes[i]
            sizes[i] *= 2
    runs, at = [], 0
    for s in sizes:
        runs.append(engines[at:at + s])
        at += s
    return runs


def _place(c, topo):
    return (topo.host(c), topo.chip(c))


def _split(j, cores, topo):
    others = [(j + k) % N for k in range(1, N)]
    far = [d for d in others if _place(cores[d], topo) != _place(cores[j], topo)]
    near = [d for d in others if _place(cores[d], topo) == _place(cores[j], topo)]
    return far, near


def _routes(cores, topo):
    routes, taken = {}, set(cores)
    for j in range(N):
        far, _ = _split(j, cores, topo)
        for i, d in enumerate(far):
            if (i + j) % 2:
                continue
            spare = [c for c in range(WORLD) if c not in taken and _place(c, topo) == _place(cores[j], topo)
                     and topo.die(c) != topo.die(cores[j]) and topo.may_write(c, cores[d])]
            if spare:
                routes[(j, d)] = spare[0]
                taken.add(spare[0])
    return routes


def _lanes(j, cores, topo, routes):
    far, near = _split(j, cores, topo)
    direct = [d for d in far if (j, d) not in routes]
    relayed = [d for d in far if (j, d) in routes]
    every = _engines(topo.mask(cores[j], cores[near[0]]))
    out = _engines(topo.mask(cores[j], cores[far[0]]))
    home = [e for e in every if e not in out]
    lanes = {}
    for group, engines in ((direct, out), (relayed, home), (near, every)):
        if group:
            for d, run in zip(group, _shares(engines, len(group))):
                lanes[d] = run
    return lanes


def rank_program(g, core, T, topo):
    cores, S, u8 = list(T.cores), T.sem, dt.uint8
    routes = _routes(cores, topo)
    r = T.rank_of(core)

    def tile(buf, i):
        return buf[:, W * i:W * i + W]

    def slot(j, at):
        return j if j < at else j - 1

    def write(src_core, dst_core, engines, sem, src, dst):
        rid, pid = topo.addr(dst_core, src_core)
        return RemoteDMATransfer(src=src, dst=dst, dst_ids=[DstId(rid=rid, pnc=pid)],
                                 dma_engine_mask=sum(1 << e for e in engines), remote_sem=sem)

    if r is None:
        for (j, d), c in routes.items():
            if c != core:
                continue
            came = len(_lanes(j, cores, topo, routes)[d])
            on = _engines(topo.mask(core, cores[d]))
            g.wait_ge(S.pa, came)
            g.remote_dma_fused([write(core, cores[d], on, S["a%d" % j], tile(T.rp, 0), tile(T.rp, slot(j, d)))],
                               local_sem=S.sent)
            g.wait_ge(S.ca, came)
            g.remote_dma_fused([write(core, cores[d], on, S["a%d" % j], tile(T.rq, 0).bitcast(u8),
                                      tile(T.rq, slot(j, d)).bitcast(u8))], local_sem=S.sent)
            g.wait_ge(S.sent, 2 * len(on))
        return

    half = N * W // 2

    g.sync.dma_start(T.wp[:], T.ws[:]).then_inc(S.ldp, 16)
    g.scalar.dma_start(T.wq[:].bitcast(u8), T.wc[:]).then_inc(S.ldc, 16)
    g.sync.dma_start(T.xb[:, 0:4 * half], T.x[:, 0:4 * half]).then_inc(S.ldx0, 16)
    g.scalar.dma_start(T.xb[:, 4 * half:8 * half], T.x[:, 4 * half:8 * half]).then_inc(S.ldx1, 16)

    far, near = _split(r, cores, topo)
    lanes = _lanes(r, cores, topo, routes)
    calls = {}
    for name, group in (("far", far), ("near", near)):
        planes, codes = [], []
        for d in group:
            if (r, d) in routes:
                to, at, sp, sc = routes[(r, d)], 0, S.pa, S.ca
            else:
                to, at, sp, sc = cores[d], slot(r, d), S["a%d" % r], S["a%d" % r]
            planes.append(write(core, to, lanes[d], sp, tile(T.wp, d), tile(T.rp, at)))
            codes.append(write(core, to, lanes[d], sc, tile(T.wq, d).bitcast(u8), tile(T.rq, at).bitcast(u8)))
        calls[name] = (planes, codes)
    left = 2 * sum(len(lanes[d]) for d in far + near)
    g.wait_ge(S.ldp, 16)
    g.remote_dma_fused(calls["far"][0], local_sem=S.sent)
    g.remote_dma_fused(calls["near"][0], local_sem=S.sent)
    g.wait_ge(S.ldc, 16)
    g.remote_dma_fused(calls["far"][1], local_sem=S.sent)
    g.remote_dma_fused(calls["near"][1], local_sem=S.sent)

    for h, (ld, q) in enumerate(((S.ldx0, S.q0), (S.ldx1, S.q1))):
        g.vector.wait_ge(ld, 16)
        g.vector.quantize_mx(T.xq[:, half * h:half * h + half], T.xp[:, half * h:half * h + half],
                             T.xb[:, 4 * half * h:4 * half * h + 4 * half]).then_inc(q, 1)

    order = [r] + near + [j for j in far if (j, r) not in routes] + [j for j in far if (j, r) in routes]
    seen = set()
    for i, j in enumerate(order):
        h = (W * j) // half
        if h not in seen:
            seen.add(h)
            g.tensor.wait_ge((S.q0, S.q1)[h], 1)
        if j == r:
            g.tensor.wait_ge(S.ldp, 16)
            g.tensor.wait_ge(S.ldc, 16)
            wq, wp = tile(T.wq, r), tile(T.wp, r)
        else:
            if (j, r) in routes:
                n = len(_engines(topo.mask(routes[(j, r)], core)))
            else:
                n = len(_lanes(j, cores, topo, routes)[r])
            g.tensor.wait_ge(S["a%d" % j], 2 * n)
            wq, wp = tile(T.rq, slot(j, r)), tile(T.rp, slot(j, r))
        mm = g.tensor.matmul_mx(T.acc[:, 0:W], wq, wp, tile(T.xq, j), tile(T.xp, j), i == 0, i == N - 1)
    mm.then_inc(S.mm, 1)

    g.vector.wait_ge(S.mm, 1)
    g.vector.tensor_copy(T.yb[:], T.acc[:, 0:W]).then_inc(S.cp, 1)
    g.sync.wait_ge(S.cp, 1)
    g.sync.dma_start(T.y[:], T.yb[:]).then_inc(S.st, 16)
    g.sync.wait_ge(S.st, 16)
    g.wait_ge(S.sent, left)
